import numpy as np
import ml_dtypes


def mxq(x, axis, fmt="e4m3"):
    dtype, down = {"e4m3": (ml_dtypes.float8_e4m3fn, 7), "e5m2": (ml_dtypes.float8_e5m2, 14)}[fmt]
    v = np.moveaxis(np.asarray(x, np.float32).astype(ml_dtypes.bfloat16).astype(np.float64), axis, -1)
    blocks = v.reshape(v.shape[:-1] + (-1, 32))
    amax = np.abs(blocks).max(-1, keepdims=True)
    byte = np.maximum(np.where(amax > 0, np.frexp(amax)[1] - 1 + 127, 0) - down, 1)
    scale = np.exp2(byte - 127.0)
    codes = (blocks / scale).astype(np.float32).astype(dtype).astype(np.float64)
    return np.moveaxis((codes * scale).reshape(v.shape), -1, axis)


WIDE = False


def mx_kscale(k):
    if not WIDE:
        return np.ones(k)
    levels = np.array([10, -10, 5, -5, 0])
    if k % 512:
        return np.exp2(np.random.permutation(np.resize(levels, k // 32))).repeat(32)
    a = np.empty((k // 512, 16))
    for p in range(k // 512):
        a[p, :8] = np.random.permutation(np.resize(levels, 8))
        for g in range(8):
            far = levels[np.abs(levels - a[p, g]) >= 10]
            a[p, g + 8] = far[np.random.randint(len(far))]
    return np.exp2(a.ravel()).repeat(32)


def f64(x):
    return np.asarray(x).astype(np.float64)


def striped(idx):
    return np.tile(idx.reshape(-1, 16).T, (8, 1)).astype(np.uint16)


def unstriped(offs):
    return offs[:16].T.reshape(-1).astype(np.int64)


def striped8(idx):
    return np.concatenate([x.reshape(-1, 16).T for x in idx]).astype(np.uint16)


def runs(offs, k):
    lists = np.stack([offs[16 * r : 16 * r + 16].T.reshape(-1) for r in range(8)]).astype(np.int64)
    return lists[np.arange(k) % 512 // 64]


def pack_weight(w):
    k, n = w.shape
    w = f64(np.asarray(w, np.float32).astype(ml_dtypes.bfloat16)).reshape(k // 32, 32, n)
    amax = np.abs(w).max(1)
    byte = np.clip(np.where(amax > 0, np.frexp(amax)[1] - 1 + 127 - 7, 1), 1, 254)
    scaled = (w * np.exp2(127.0 - byte)[:, None, :]).reshape(k, n).astype(np.float32)
    words = np.ascontiguousarray(scaled.reshape(k // 512, 128, 4, n).transpose(0, 1, 3, 2)).astype(ml_dtypes.float8_e4m3fn).view(np.uint8)
    return words, np.ascontiguousarray(byte.astype(np.uint8).reshape(k // 512, 16, n))


def unpack_weight(words, scales):
    g, p, n, _ = words.shape
    vals = np.ascontiguousarray(words).view(ml_dtypes.float8_e4m3fn).astype(np.float64) * np.repeat(np.exp2(scales.astype(np.float64) - 127.0), 8, axis=1)[..., None]
    return vals.transpose(0, 1, 3, 2).reshape(g * 512, n)


K, T, S, V, N, H = 512, 2048, 512, 256, 512, 512


def setup_inputs():
    n = np.random.standard_normal
    s = mx_kscale(K)[:, None]
    u = mx_kscale(H)
    packed_xT = pack_weight(n((K, T)) * s)
    return {
        "x_words": packed_xT[0],
        "x_scales": packed_xT[1],
        "w1": (n((K, H)) / np.sqrt(K) / s * u).astype(np.float32),
        "w2": (n((H, H)) / np.sqrt(H) / u[:, None] * u).astype(np.float32),
        "w3": (n((H, N)) / np.sqrt(H) / u[:, None]).astype(np.float32),
        "res": (2 * n((N, S))).astype(np.float32),
        "offs": striped(np.random.permutation(T)[:S]),
        "src": striped8(np.stack([np.random.permutation(S)[:V] for _ in range(8)])),
        "dst": striped8(np.stack([np.random.permutation(S)[:V] for _ in range(8)])),
        "back": striped8(np.stack([np.random.permutation(S) for _ in range(8)])),
    }


def reference(x_words, x_scales, w1, w2, w3, res, offs, src, dst, back):
    xq = unpack_weight(x_words, x_scales)[:, unstriped(offs)]
    y = mxq(f64(w1), 0, "e4m3").T @ xq
    m1 = np.maximum(y[np.arange(H)[:, None], runs(src, H)], y[np.arange(H)[:, None], runs(dst, H)])
    z = y.copy()
    z[np.arange(H)[:, None], runs(dst, H)] = m1
    h = mxq(f64(w2), 0, "e4m3").T @ mxq(z, 0, "e4m3")
    z2 = h - (h[np.arange(H)[:, None], runs(back, H)])
    return f64(res) + (mxq(f64(w3), 0, "e4m3").T @ mxq(z2, 0, "e4m3"))

from contextlib import ExitStack

import concourse.mybir as mybir

K, T, S, V, N, H = 512, 2048, 512, 256, 512, 512
FLOPS = 3 * 2 * 512 * 512 * 512

F32 = mybir.dt.float32
BF16 = mybir.dt.bfloat16
I32 = mybir.dt.int32
U32 = mybir.dt.uint32
U16 = mybir.dt.uint16
U8 = mybir.dt.uint8
FP8X4 = mybir.dt.float8_e4m3fn_x4
COPY = mybir.ActivationFunctionType.Copy
ALU = mybir.AluOpType

P = 128
HALF = S // 2
PLANE_ORDER = (2, 0, 1, 3)
PIECES = ((0, 256), (256, 128), (384, 128))


def tile_picked_maxinto_none_p_kernel(
    tc, x_words, x_scales, w1, w2, w3, res, offs, src, dst, back, out
):
    nc = tc.nc
    with ExitStack() as ctx:
        keep = ctx.enter_context(tc.tile_pool(name="keep", bufs=1))
        psum = ctx.enter_context(tc.psum_pool(name="psum", bufs=1))

        def sb(name, shape, dtype, tag=None):
            return keep.tile(shape, dtype, name=name, tag=tag or name, align_bytes=64)

        def bank(name, b, shape):
            return psum.tile(shape, F32, name=name, tag="bank%d" % b)

        def quantize(codes, scales, values):
            nc.vector.quantize_mx(out=codes.bitcast(FP8X4), scales=scales, in_=values)

        def product(acc, w_codes, w_scales, codes, scales):
            nc.tensor.matmul_mx(out=acc, lhsT=w_codes.bitcast(FP8X4), lhsT_scale=w_scales,
                                rhs=codes.bitcast(FP8X4), rhs_scale=scales, start=True, stop=True)

        offs_t = sb("offs_t", [P, S // 16], U16)
        src_t = sb("src_t", [P, V // 16], U16)
        dst_t = sb("dst_t", [P, V // 16], U16)
        back_t = sb("back_t", [P, S // 16], U16)
        xw = sb("xw", [P, T], U32)
        xs = sb("xs", [P, T], U8)
        w1_raw = [sb("w1_raw%d" % h, [P, 4, 256], F32, tag="raw%d" % h) for h in range(2)]
        w1_v = w1.rearrange("(p j) c -> p j c", j=4)

        nc.vector.memset(xs[:].bitcast(I32), 0)
        for q in range(4):
            nc.scalar.dma_start(xs[32 * q : 32 * q + 4, :].bitcast(I32), x_scales[0, 4 * q : 4 * q + 4, :].bitcast(I32))
        nc.sync.dma_start(offs_t[:], offs)
        nc.sync.dma_start(src_t[:], src)
        nc.sync.dma_start(dst_t[:], dst)
        nc.sync.dma_start(xw[:].bitcast(I32), x_words[0].rearrange("p n r -> p (n r)").bitcast(I32))
        for h in range(2):
            nc.sync.dma_start(w1_raw[h][:], w1_v[:, :, 256 * h : 256 * h + 256])
        nc.sync.dma_start(back_t[:], back)

        def deal(copy, dealt, raw, pair):
            copy(dealt[:].rearrange("p t m j -> p m j t"),
                 raw[:].rearrange("p j (m t) -> p m j t", t=4)[:, :, :, 2 * pair : 2 * pair + 2])

        xw_g = [sb("xw_g%d" % h, [P, HALF], U32) for h in range(2)]
        for h in range(2):
            nc.vector.tensor_copy(xw_g[h][:], xw[:].indirect(offs_t[:, 16 * h : 16 * h + 16]))
        xs_g = sb("xs_g", [P, S], U8, tag="xw")
        nc.vector.tensor_copy(xs_g[:], xs[:].indirect(offs_t[:]))

        w1_codes = [sb("w1_codes%d" % t, [P, P], U32) for t in range(4)]
        w1_scales = [sb("w1_scales%d" % t, [P, P], U8) for t in range(4)]
        first_pair = PLANE_ORDER[0] // 2
        w1_bf = {}
        for h in range(2):
            for pair in (first_pair, 1 - first_pair):
                w1_bf[h, pair] = sb("w1_bf%d%d" % (h, pair), [P, 2, 64, 4], BF16)
                on_vector = h == 1 and pair == first_pair
                deal(nc.vector.tensor_copy if on_vector else nc.scalar.copy, w1_bf[h, pair], w1_raw[h], pair)

        def quantize_w1(t):
            for h in range(2):
                quantize(w1_codes[t][:, 64 * h : 64 * h + 64], w1_scales[t][:, 64 * h : 64 * h + 64],
                         w1_bf[h, t // 2][:, t % 2].rearrange("p m j -> p (m j)"))

        w2_raw = sb("w2_raw", [P, 4, H], F32, tag="raw0")
        nc.sync.dma_start(w2_raw[:], w2.rearrange("(p j) c -> p j c", j=4))
        w3_v = w3.rearrange("(p j) c -> p j c", j=4)
        w3_raw = [sb("w3_raw0", [P, 4, 256], F32, tag="raw1")]
        nc.sync.dma_start(w3_raw[0][:], w3_v[:, :, 0:256])

        y = {}
        for t in PLANE_ORDER:
            quantize_w1(t)
            y[t] = sb("y%d" % t, [P, S], F32)
            for h in range(2):
                acc = bank("y_acc%d%d" % (t, h), 2 * t + h, [P, HALF])
                product(acc[:], w1_codes[t][:], w1_scales[t][:], xw_g[h][:], xs_g[:, HALF * h : HALF * (h + 1)])
                nc.scalar.copy(y[t][:, HALF * h : HALF * (h + 1)], acc[:])

        w3_raw.append(sb("w3_raw1", [P, 4, 256], F32, tag="xw"))
        nc.sync.dma_start(w3_raw[1][:], w3_v[:, :, 256:512])
        w2_bf = [sb("w2_bf%d" % u, [P, 2, P, 4], BF16) for u in range(2)]
        w3_bf = [sb("w3_bf%d" % u, [P, 256, 4], BF16) for u in range(2)]

        def interleave_w3(u):
            nc.scalar.copy(w3_bf[u][:].rearrange("p (c i) j -> p c j i", i=4),
                           w3_raw[u][:].rearrange("p j (c i) -> p c j i", i=4))

        for u in range(2):
            deal(nc.scalar.copy, w2_bf[u], w2_raw, u)
        res_t = sb("res_t", [P, 4, S], F32, tag="raw0")
        nc.sync.dma_start(res_t[:], res.rearrange("(t p) j -> p t j", p=P))

        for u in range(2):
            interleave_w3(u)
        z_bf = [sb("z_bf%d" % h, [P, HALF, 4], BF16, tag=("raw1", "xw")[h]) for h in range(2)]
        picked = {}

        def fetch(t):
            picked[t] = sb("picked%d" % t, [P, 2, V], F32)
            nc.vector.tensor_copy(picked[t][:, 0, :], y[t][:].indirect(src_t[:]))
            nc.vector.tensor_copy(picked[t][:, 1, :], y[t][:].indirect(dst_t[:]))

        def put(t):
            tag = "y%d" % PLANE_ORDER[0] if t == PLANE_ORDER[-1] else None
            m1 = sb("m1_%d" % t, [P, V], F32, tag=tag)
            nc.vector.tensor_tensor(m1[:], picked[t][:, 0, :], picked[t][:, 1, :], ALU.max)
            nc.vector.tensor_copy(y[t][:].indirect(dst_t[:]), m1[:])

        def round_z(t):
            for h in range(2):
                if t != PLANE_ORDER[-1]:
                    nc.scalar.copy(z_bf[h][:, :, t], y[t][:, HALF * h : HALF * (h + 1)])
                else:
                    nc.scalar.copy(z_bf[h][:, 0:P, t], y[t][:, HALF * h : HALF * h + P])
                    nc.vector.tensor_copy(z_bf[h][:, P:HALF, t], y[t][:, HALF * h + P : HALF * (h + 1)])

        w2_codes = {}
        w2_scales = {}

        def quantize_w2(t):
            quantize(w2_codes[t], w2_scales[t], w2_bf[t // 2][:, t % 2].rearrange("p m j -> p (m j)"))

        w2_codes_first = sb("w2_codes_first", [P, P], U32)
        w2_scales_t = sb("w2_scales", [P, H], U8)
        w2_codes[0] = w2_codes_first[:]
        for t in range(4):
            w2_scales[t] = w2_scales_t[:, P * t : P * (t + 1)]

        fetch(PLANE_ORDER[0])
        for i, t in enumerate(PLANE_ORDER):
            if i + 1 < 4:
                fetch(PLANE_ORDER[i + 1])
            put(t)
            if i == 3:
                quantize_w2(0)
            round_z(t)

        z_codes = [sb("z_codes%d" % h, [P, HALF], U32) for h in range(2)]
        z_scales = [sb("z_scales%d" % h, [P, HALF], U8) for h in range(2)]
        for h in range(2):
            quantize(z_codes[h][:], z_scales[h][:], z_bf[h][:].rearrange("p c t -> p (c t)"))
        w2_codes_rest = sb("w2_codes_rest", [P, 3 * P], U32, tag="xw")
        for t in range(1, 4):
            w2_codes[t] = w2_codes_rest[:, P * (t - 1) : P * t]
        quantize_w2(1)
        quantize(w2_codes_rest[:, P : 3 * P], w2_scales_t[:, 2 * P : 4 * P], w2_bf[1][:].rearrange("p t m j -> p (t m j)"))

        hwin = {}
        hplain = [sb("hplain%d" % h, [P, 4, HALF], F32) for h in range(2)]
        h_acc = {}
        for t in range(4):
            hwin[t] = sb("hwin%d" % t, [P, S], F32)
            for h in range(2):
                h_acc[t, h] = bank("h_acc%d%d" % (t, h), 2 * t + h, [P, HALF])
                product(h_acc[t, h][:], w2_codes[t], w2_scales[t], z_codes[h][:], z_scales[h][:])
                nc.scalar.copy(hwin[t][:, HALF * h : HALF * (h + 1)], h_acc[t, h][:])
            (nc.vector.tensor_copy if t == 0 else nc.scalar.copy)(hplain[0][:, t, :], h_acc[t, 0][:])
        for t in range(4):
            nc.scalar.copy(hplain[1][:, t, :], h_acc[t, 1][:])

        w3_codes = [sb("w3_codes%d" % u, [P, 256], U32, tag="z_codes%d" % u) for u in range(2)]
        w3_scales = [sb("w3_scales%d" % u, [P, 256], U8) for u in range(2)]
        out_v = out.rearrange("(t p) j -> p t j", p=P)

        z2_bf = {}

        def fetch_back(n):
            c0, w = PIECES[n]
            diff = sb("diff%d" % n, [P, 4, w], F32)
            for t in range(4):
                nc.vector.tensor_tensor(diff[:, t, :], hwin[t][:].indirect(back_t[:, c0 // 16 : (c0 + w) // 16]),
                                        hplain[c0 // HALF][:, t, c0 % HALF : c0 % HALF + w], ALU.subtract)
                if n == 0 and t in (1, 2):
                    quantize(w3_codes[t - 1][:], w3_scales[t - 1][:], w3_bf[t - 1][:].rearrange("p c j -> p (c j)"))
            z2_bf[n] = sb("z2_bf%d" % n, [P, w, 4], BF16)
            nc.scalar.activation(z2_bf[n][:].rearrange("p (c i) t -> p c t i", i=4),
                                 diff[:].rearrange("p t (c i) -> p c t i", i=4), COPY, scale=-1.0)

        o_acc = {}

        def last_product(n):
            c0, w = PIECES[n]
            codes = sb("z2_codes%d" % n, [P, w], U32)
            scales = sb("z2_scales%d" % n, [P, w], U8)
            quantize(codes[:], scales[:], z2_bf[n][:].rearrange("p c t -> p (c t)"))
            for u in range(2):
                o_acc[n, u] = bank("o_acc%d%d" % (n, u), 2 * n + u, [P, 2, w])
                for e in range(2):
                    product(o_acc[n, u][:, e, :], w3_codes[u][:, P * e : P * (e + 1)], w3_scales[u][:, P * e : P * (e + 1)],
                            codes[:], scales[:])

        def finish(n):
            c0, w = PIECES[n]
            for u in range(2):
                o = sb("o%d%d" % (n, u), [P, 2, w], F32)
                nc.vector.tensor_tensor(o[:], o_acc[n, u][:], res_t[:, 2 * u : 2 * u + 2, c0 : c0 + w], ALU.add)
                nc.sync.dma_start(out_v[:, 2 * u : 2 * u + 2, c0 : c0 + w], o[:])

        fetch_back(0)
        fetch_back(1)
        last_product(0)
        fetch_back(2)
        last_product(1)
        finish(0)
        last_product(2)
        finish(1)
        finish(2)
